import numpy as np
import ml_dtypes


def mxq(x, axis, fmt="e4m3"):
    dtype, down = {"e4m3": (ml_dtypes.float8_e4m3fn, 7), "e5m2": (ml_dtypes.float8_e5m2, 14)}[fmt]
    v = np.moveaxis(np.asarray(x, np.float32).astype(ml_dtypes.bfloat16).astype(np.float64), axis, -1)
    blocks = v.reshape(v.shape[:-1] + (-1, 32))
    amax = np.abs(blocks).max(-1, keepdims=True)
    byte = np.maximum(np.where(amax > 0, np.frexp(amax)[1] - 1 + 127, 0) - down, 1)
    scale = np.exp2(byte - 127.0)
    codes = (blocks / scale).astype(np.float32).astype(dtype).astype(np.float64)
    return np.moveaxis((codes * scale).reshape(v.shape), -1, axis)


WIDE = False


def mx_kscale(k):
    if not WIDE:
        return np.ones(k)
    levels = np.array([10, -10, 5, -5, 0])
    if k % 512:
        return np.exp2(np.random.permutation(np.resize(levels, k // 32))).repeat(32)
    a = np.empty((k // 512, 16))
    for p in range(k // 512):
        a[p, :8] = np.random.permutation(np.resize(levels, 8))
        for g in range(8):
            far = levels[np.abs(levels - a[p, g]) >= 10]
            a[p, g + 8] = far[np.random.randint(len(far))]
    return np.exp2(a.ravel()).repeat(32)


def f64(x):
    return np.asarray(x).astype(np.float64)


def striped(idx):
    return np.tile(np.asarray(idx).reshape(-1, 16).T, (8, 1)).astype(np.uint16)


def unstriped(offs):
    return offs[:16].T.reshape(-1).astype(np.int64)


E2M1 = np.array([0.0, 0.5, 1.0, 1.5, 2.0, 3.0, 4.0, 6.0, -0.0, -0.5, -1.0, -1.5, -2.0, -3.0, -4.0, -6.0])


def pack_weight(w, fmt):
    k, n = w.shape
    w = f64(np.asarray(w, np.float32).astype(ml_dtypes.bfloat16)).reshape(k // 32, 32, n)
    amax = np.abs(w).max(1)
    if fmt == "e4m3":
        byte = np.frexp(amax)[1] - 1 + 127 - 7
    else:
        mant, ex = np.frexp(amax / 6.0)
        byte = np.where(mant > 0.5, ex, ex - 1) + 127
    byte = np.clip(np.where(amax > 0, byte, 1), 1, 254)
    scaled = (w * np.exp2(127.0 - byte)[:, None, :]).reshape(k, n).astype(np.float32)
    by_word = np.ascontiguousarray(scaled.reshape(k // 512, 128, 4, n).transpose(0, 1, 3, 2))
    if fmt == "e4m3":
        words = by_word.astype(ml_dtypes.float8_e4m3fn).view(np.uint8)
    else:
        c = by_word.astype(ml_dtypes.float4_e2m1fn).view(np.uint8) & 0xF
        words = (c[..., 0::2] | (c[..., 1::2] << 4)).reshape(k // 512, 128, 2 * n)
    return np.ascontiguousarray(words), np.ascontiguousarray(byte.astype(np.uint8).reshape(k // 512, 16, n))


def unpack_weight(words, scales, fmt):
    g, _, n = scales.shape
    words = np.ascontiguousarray(words).reshape(g, 128, n, -1)
    if fmt == "e4m3":
        vals = words.view(ml_dtypes.float8_e4m3fn).astype(np.float64)
    else:
        nib = np.empty((g, 128, n, 4), np.uint8)
        nib[..., 0::2] = words & 0xF
        nib[..., 1::2] = words >> 4
        vals = E2M1[nib]
    vals = vals * np.repeat(np.exp2(scales.astype(np.float64) - 127.0), 8, axis=1)[..., None]
    return vals.transpose(0, 1, 3, 2).reshape(g * 512, n)


C, I, T, N, L = 2048, 512, 512, 512, 512


def setup_inputs():
    n = np.random.standard_normal
    idx = np.random.permutation(C)[:I]
    fi = mx_kscale(I)
    fl = mx_kscale(L)
    ti = np.ones(C)
    ti[idx] = fi
    cxp = pack_weight(n((L, T)) / fl[:, None], "e2m1")
    wcp = pack_weight(n((L, N)) * 1 / np.sqrt(L) * fl[:, None], "e4m3")
    return {
        "xt": (n((T, C)) / ti).astype(np.float32),
        "wt": (n((N, C)) * (1 / np.sqrt(I)) * ti).astype(np.float32),
        "cx_words": cxp[0],
        "cx_scales": cxp[1],
        "wc_words": wcp[0],
        "wc_scales": wcp[1],
        "offs": striped(idx),
    }


def reference(xt, wt, cx_words, cx_scales, wc_words, wc_scales, offs):
    idx = unstriped(offs)
    cxu = unpack_weight(cx_words, cx_scales, "e2m1")
    wcu = unpack_weight(wc_words, wc_scales, "e4m3")
    xs = f64(xt)[:, idx].T
    ws1 = f64(wt)[:, idx].T
    ws1q = mxq(ws1, 0, "e4m3")
    xsq = mxq(xs, 0, "e4m3")
    y = ws1q.T @ xsq + wcu.T @ cxu
    return y

@@ -1,0 +1,138 @@
+from contextlib import ExitStack
+
+import concourse.mybir as mybir
+from concourse.masks import make_identity
+
+F32 = mybir.dt.float32
+BF16 = mybir.dt.bfloat16
+I32 = mybir.dt.int32
+U32 = mybir.dt.uint32
+U16 = mybir.dt.uint16
+U8 = mybir.dt.uint8
+E4M3 = mybir.dt.float8_e4m3fn_x4
+E2M1 = mybir.dt.float4_e2m1fn_x4
+
+P = 128
+C, I, T, N, L = 2048, 512, 512, 512, 512
+BLOCKS = 4
+FLOPS = 2 * N * T * (I + L)
+
+
+def tile_list_pruned_inputs_kernel(tc, xt, wt, cx_words, cx_scales, wc_words, wc_scales, offs, out):
+    nc = tc.nc
+    with ExitStack() as ctx:
+        keep = ctx.enter_context(tc.tile_pool(name="keep", bufs=1))
+        ring = ctx.enter_context(tc.tile_pool(name="ring", bufs=2))
+        turn = ctx.enter_context(tc.psum_pool(name="turn", bufs=2))
+        sums = ctx.enter_context(tc.psum_pool(name="sums", bufs=1))
+
+        offsets = keep.tile([P, I // 16], U16, name="offsets")
+        x_rows = [keep.tile([P, C], F32, name="x_rows%d" % b) for b in range(BLOCKS)]
+        w_rows = [keep.tile([P, C], F32, name="w_rows%d" % b) for b in range(BLOCKS)]
+        cx_codes = keep.tile([P, 2 * T], U8, name="cx_codes", align_bytes=64)
+        wc_codes = keep.tile([P, 4 * N], U8, name="wc_codes", align_bytes=64)
+        cx_plane = keep.tile([P, T], U8, name="cx_plane", align_bytes=64)
+        wc_plane = keep.tile([P, N], U8, name="wc_plane", align_bytes=64)
+        ident = keep.tile([P, P], F32, name="ident")
+
+        make_identity(nc, ident[:])
+
+        def load_scale_rows(plane, rows, q):
+            nc.sync.dma_start(plane[32 * q : 32 * q + 4, :].bitcast(I32), rows[0, 4 * q : 4 * q + 4, :].bitcast(I32))
+
+        nc.sync.dma_start(x_rows[0][:], xt[0:P, :])
+        nc.sync.dma_start(offsets[:], offs)
+        for b in range(1, BLOCKS):
+            nc.sync.dma_start(x_rows[b][:], xt[b * P : (b + 1) * P, :])
+            load_scale_rows(cx_plane, cx_scales, b - 1)
+        for b in range(BLOCKS - 1):
+            nc.sync.dma_start(w_rows[b][:], wt[b * P : (b + 1) * P, :])
+            if b == 0:
+                load_scale_rows(cx_plane, cx_scales, 3)
+            else:
+                load_scale_rows(wc_plane, wc_scales, b - 1)
+        nc.sync.dma_start(cx_codes[:].bitcast(I32), cx_words[0].bitcast(I32))
+        load_scale_rows(wc_plane, wc_scales, 2)
+        load_scale_rows(wc_plane, wc_scales, 3)
+        nc.sync.dma_start(wc_codes[:].bitcast(I32), wc_words[0].rearrange("p n r -> p (n r)").bitcast(I32))
+        nc.sync.dma_start(w_rows[BLOCKS - 1][:], wt[(BLOCKS - 1) * P :, :])
+
+        def make_operand(row_tiles, codes, plane):
+            grouped = ring.tile([P, len(row_tiles) * 4 * P], BF16, name="grouped", align_bytes=64)
+            for j, rows in enumerate(row_tiles):
+                picked = ring.tile([P, I], BF16, name="picked")
+                nc.vector.tensor_copy(picked[:], rows[:].indirect(offsets[:]))
+                pairs = picked[:].bitcast(F32)
+                turned = turn.tile([P, 2, P], F32, name="turned")
+                for u in range(2):
+                    nc.tensor.transpose(turned[:, u, :], pairs[:, u : 2 * P : 2], ident[:])
+                nc.scalar.copy(
+                    grouped[:, j * 4 * P : (j + 1) * 4 * P].bitcast(F32).rearrange("p (r u) -> p r u", u=2),
+                    turned[:].rearrange("p u r -> p r u"),
+                )
+            nc.vector.quantize_mx(out=codes.bitcast(E4M3), scales=plane, in_=grouped[:])
+
+        codes = keep.tile([P, T + N], U32, name="codes", align_bytes=64)
+        plane = keep.tile([P, T + N], U8, name="plane", align_bytes=64)
+        row_tiles = x_rows + w_rows
+
+        def quantise(b0, b1):
+            make_operand(row_tiles[b0:b1], codes[:, b0 * P : b1 * P], plane[:, b0 * P : b1 * P])
+
+        def context_pass(acc, b, t0, t1, start, stop):
+            nc.tensor.matmul_mx(
+                out=acc,
+                lhsT=wc_codes[:, 4 * b * P : 4 * (b + 1) * P].bitcast(E4M3),
+                lhsT_scale=wc_plane[:, b * P : (b + 1) * P],
+                rhs=cx_codes[:, 2 * t0 : 2 * t1].bitcast(E2M1),
+                rhs_scale=cx_plane[:, t0:t1],
+                start=start,
+                stop=stop,
+            )
+
+        def picked_pass(acc, b, t0, t1, start):
+            nc.tensor.matmul_mx(
+                out=acc,
+                lhsT=codes[:, T + b * P : T + (b + 1) * P].bitcast(E4M3),
+                lhsT_scale=plane[:, T + b * P : T + (b + 1) * P],
+                rhs=codes[:, t0:t1].bitcast(E4M3),
+                rhs_scale=plane[:, t0:t1],
+                start=start,
+                stop=not start,
+            )
+
+        def store_block(acc, b):
+            result = keep.tile([P, T], F32, name="result%d" % b)
+            nc.scalar.copy(result[:], acc[:])
+            nc.sync.dma_start(out[b * P : (b + 1) * P, :], result[:])
+
+        accs = [sums.tile([P, T], F32, name="acc%d" % b) for b in range(BLOCKS - 1)]
+        half = T // 2
+        last = BLOCKS - 1
+        halves = [sums.tile([P, half], F32, name="acc_half%d" % h) for h in range(2)]
+        quantise(0, 1)
+        quantise(1, 3)
+        quantise(3, 5)
+        picked_pass(accs[0][:], 0, 0, T, True)
+        quantise(5, 7)
+        context_pass(accs[0][:], 0, 0, T, False, True)
+        store_block(accs[0], 0)
+        for b in range(1, last):
+            context_pass(accs[b][:], b, 0, T, True, False)
+        for h in range(2):
+            for s in range(2):
+                t0 = h * half + s * P
+                context_pass(halves[h][:, s * P : (s + 1) * P], last, t0, t0 + P, s == 0, False)
+        for b in range(1, last):
+            picked_pass(accs[b][:], b, 0, T, False)
+            store_block(accs[b], b)
+        quantise(7, 8)
+        for h in range(2):
+            picked_pass(halves[h][:], last, h * half, (h + 1) * half, False)
+            result = keep.tile([P, half], F32, name="result_half%d" % h)
+            if h == 0:
+                nc.vector.tensor_copy(result[:], halves[h][:])
+                nc.sync.dma_start(out[last * P :, 0:half], result[:])
+            else:
+                nc.scalar.copy(result[:], halves[h][:])
+                nc.scalar.dma_start(out[last * P :, half:T], result[:])

@@ -37,35 +37,38 @@ def tile_list_pruned_inputs_kernel(tc, xt, wt, cx_words, cx_scales, wc_words, wc
 
         make_identity(nc, ident[:])
 
-        def load_scale_rows(plane, rows, q):
-            nc.sync.dma_start(plane[32 * q : 32 * q + 4, :].bitcast(I32), rows[0, 4 * q : 4 * q + 4, :].bitcast(I32))
+        def load_rows(tile, source, b):
+            nc.sync.dma_start(tile[:], source[b * P : (b + 1) * P, :])
 
-        nc.sync.dma_start(x_rows[0][:], xt[0:P, :])
+        def load_scale_rows(scale_plane, scale_rows):
+            for q in range(4):
+                nc.sync.dma_start(
+                    scale_plane[32 * q : 32 * q + 4, :].bitcast(I32), scale_rows[0, 4 * q : 4 * q + 4, :].bitcast(I32)
+                )
+
+        load_rows(x_rows[0], xt, 0)
         nc.sync.dma_start(offsets[:], offs)
-        for b in range(1, BLOCKS):
-            nc.sync.dma_start(x_rows[b][:], xt[b * P : (b + 1) * P, :])
-            load_scale_rows(cx_plane, cx_scales, b - 1)
-        for b in range(BLOCKS - 1):
-            nc.sync.dma_start(w_rows[b][:], wt[b * P : (b + 1) * P, :])
-            if b == 0:
-                load_scale_rows(cx_plane, cx_scales, 3)
-            else:
-                load_scale_rows(wc_plane, wc_scales, b - 1)
+        load_rows(x_rows[1], xt, 1)
+        load_scale_rows(cx_plane, cx_scales)
+        load_rows(x_rows[2], xt, 2)
+        load_rows(x_rows[3], xt, 3)
+        load_rows(w_rows[0], wt, 0)
+        load_scale_rows(wc_plane, wc_scales)
+        load_rows(w_rows[1], wt, 1)
+        load_rows(w_rows[2], wt, 2)
         nc.sync.dma_start(cx_codes[:].bitcast(I32), cx_words[0].bitcast(I32))
-        load_scale_rows(wc_plane, wc_scales, 2)
-        load_scale_rows(wc_plane, wc_scales, 3)
         nc.sync.dma_start(wc_codes[:].bitcast(I32), wc_words[0].rearrange("p n r -> p (n r)").bitcast(I32))
-        nc.sync.dma_start(w_rows[BLOCKS - 1][:], wt[(BLOCKS - 1) * P :, :])
+        load_rows(w_rows[3], wt, 3)
 
         def make_operand(row_tiles, codes, plane):
             grouped = ring.tile([P, len(row_tiles) * 4 * P], BF16, name="grouped", align_bytes=64)
             for j, rows in enumerate(row_tiles):
                 picked = ring.tile([P, I], BF16, name="picked")
-                nc.vector.tensor_copy(picked[:], rows[:].indirect(offsets[:]))
+                nc.vector.tensor_copy(picked[:].rearrange("p (u g e) -> p g u e", u=2, e=16), rows[:].indirect(offsets[:]))
                 pairs = picked[:].bitcast(F32)
                 turned = turn.tile([P, 2, P], F32, name="turned")
                 for u in range(2):
-                    nc.tensor.transpose(turned[:, u, :], pairs[:, u : 2 * P : 2], ident[:])
+                    nc.tensor.transpose(turned[:, u, :], pairs[:, u * P : (u + 1) * P], ident[:])
                 nc.scalar.copy(
                     grouped[:, j * 4 * P : (j + 1) * 4 * P].bitcast(F32).rearrange("p (r u) -> p r u", u=2),
                     turned[:].rearrange("p u r -> p r u"),

@@ -30,7 +30,7 @@ def tile_list_pruned_inputs_kernel(tc, xt, wt, cx_words, cx_scales, wc_words, wc
         x_rows = [keep.tile([P, C], F32, name="x_rows%d" % b) for b in range(BLOCKS)]
         w_rows = [keep.tile([P, C], F32, name="w_rows%d" % b) for b in range(BLOCKS)]
         cx_codes = keep.tile([P, 2 * T], U8, name="cx_codes", align_bytes=64)
-        wc_codes = keep.tile([P, 4 * N], U8, name="wc_codes", align_bytes=64)
+        wc_codes = [keep.tile([P, 2 * N], U8, name="wc_codes%d" % h, align_bytes=64) for h in range(2)]
         cx_plane = keep.tile([P, T], U8, name="cx_plane", align_bytes=64)
         wc_plane = keep.tile([P, N], U8, name="wc_plane", align_bytes=64)
         ident = keep.tile([P, P], F32, name="ident")
@@ -57,8 +57,10 @@ def tile_list_pruned_inputs_kernel(tc, xt, wt, cx_words, cx_scales, wc_words, wc
         load_rows(w_rows[1], wt, 1)
         load_rows(w_rows[2], wt, 2)
         nc.sync.dma_start(cx_codes[:].bitcast(I32), cx_words[0].bitcast(I32))
-        nc.sync.dma_start(wc_codes[:].bitcast(I32), wc_words[0].rearrange("p n r -> p (n r)").bitcast(I32))
+        wc_flat = wc_words[0].rearrange("p n r -> p (n r)")
+        nc.sync.dma_start(wc_codes[0][:].bitcast(I32), wc_flat[:, 0 : 2 * N].bitcast(I32))
         load_rows(w_rows[3], wt, 3)
+        nc.sync.dma_start(wc_codes[1][:].bitcast(I32), wc_flat[:, 2 * N :].bitcast(I32))
 
         def make_operand(row_tiles, codes, plane):
             grouped = ring.tile([P, len(row_tiles) * 4 * P], BF16, name="grouped", align_bytes=64)
@@ -85,7 +87,7 @@ def tile_list_pruned_inputs_kernel(tc, xt, wt, cx_words, cx_scales, wc_words, wc
         def context_pass(acc, b, t0, t1, start, stop):
             nc.tensor.matmul_mx(
                 out=acc,
-                lhsT=wc_codes[:, 4 * b * P : 4 * (b + 1) * P].bitcast(E4M3),
+                lhsT=wc_codes[b // 2][:, 4 * (b % 2) * P : 4 * (b % 2 + 1) * P].bitcast(E4M3),
                 lhsT_scale=wc_plane[:, b * P : (b + 1) * P],
                 rhs=cx_codes[:, 2 * t0 : 2 * t1].bitcast(E2M1),
                 rhs_scale=cx_plane[:, t0:t1],
@@ -120,16 +122,17 @@ def tile_list_pruned_inputs_kernel(tc, xt, wt, cx_words, cx_scales, wc_words, wc
         quantise(5, 7)
         context_pass(accs[0][:], 0, 0, T, False, True)
         store_block(accs[0], 0)
-        for b in range(1, last):
-            context_pass(accs[b][:], b, 0, T, True, False)
+        context_pass(accs[1][:], 1, 0, T, True, False)
+        picked_pass(accs[1][:], 1, 0, T, False)
+        store_block(accs[1], 1)
+        picked_pass(accs[2][:], 2, 0, T, True)
+        quantise(7, 8)
         for h in range(2):
             for s in range(2):
                 t0 = h * half + s * P
                 context_pass(halves[h][:, s * P : (s + 1) * P], last, t0, t0 + P, s == 0, False)
-        for b in range(1, last):
-            picked_pass(accs[b][:], b, 0, T, False)
-            store_block(accs[b], b)
-        quantise(7, 8)
+        context_pass(accs[2][:], 2, 0, T, False, True)
+        store_block(accs[2], 2)
         for h in range(2):
             picked_pass(halves[h][:], last, h * half, (h + 1) * half, False)
             result = keep.tile([P, half], F32, name="result_half%d" % h)

@@ -127,12 +127,12 @@ def tile_list_pruned_inputs_kernel(tc, xt, wt, cx_words, cx_scales, wc_words, wc
         store_block(accs[1], 1)
         picked_pass(accs[2][:], 2, 0, T, True)
         quantise(7, 8)
+        context_pass(accs[2][:], 2, 0, T, False, True)
+        store_block(accs[2], 2)
         for h in range(2):
             for s in range(2):
                 t0 = h * half + s * P
                 context_pass(halves[h][:, s * P : (s + 1) * P], last, t0, t0 + P, s == 0, False)
-        context_pass(accs[2][:], 2, 0, T, False, True)
-        store_block(accs[2], 2)
         for h in range(2):
             picked_pass(halves[h][:], last, h * half, (h + 1) * half, False)
             result = keep.tile([P, half], F32, name="result_half%d" % h)

from contextlib import ExitStack

import concourse.mybir as mybir
from concourse.masks import make_identity

F32 = mybir.dt.float32
BF16 = mybir.dt.bfloat16
I32 = mybir.dt.int32
U32 = mybir.dt.uint32
U16 = mybir.dt.uint16
U8 = mybir.dt.uint8
E4M3 = mybir.dt.float8_e4m3fn_x4
E2M1 = mybir.dt.float4_e2m1fn_x4

P = 128
C, I, T, N, L = 2048, 512, 512, 512, 512
BLOCKS = 4
FLOPS = 2 * N * T * (I + L)


def tile_list_pruned_inputs_kernel(tc, xt, wt, cx_words, cx_scales, wc_words, wc_scales, offs, out):
    nc = tc.nc
    with ExitStack() as ctx:
        keep = ctx.enter_context(tc.tile_pool(name="keep", bufs=1))
        ring = ctx.enter_context(tc.tile_pool(name="ring", bufs=2))
        turn = ctx.enter_context(tc.psum_pool(name="turn", bufs=2))
        sums = ctx.enter_context(tc.psum_pool(name="sums", bufs=1))

        offsets = keep.tile([P, I // 16], U16, name="offsets")
        x_rows = [keep.tile([P, C], F32, name="x_rows%d" % b) for b in range(BLOCKS)]
        w_rows = [keep.tile([P, C], F32, name="w_rows%d" % b) for b in range(BLOCKS)]
        cx_codes = keep.tile([P, 2 * T], U8, name="cx_codes", align_bytes=64)
        wc_codes = [keep.tile([P, 2 * N], U8, name="wc_codes%d" % h, align_bytes=64) for h in range(2)]
        cx_plane = keep.tile([P, T], U8, name="cx_plane", align_bytes=64)
        wc_plane = keep.tile([P, N], U8, name="wc_plane", align_bytes=64)
        ident = keep.tile([P, P], F32, name="ident")

        make_identity(nc, ident[:])

        def load_rows(tile, source, b):
            nc.sync.dma_start(tile[:], source[b * P : (b + 1) * P, :])

        def load_scale_rows(scale_plane, scale_rows):
            for q in range(4):
                nc.sync.dma_start(
                    scale_plane[32 * q : 32 * q + 4, :].bitcast(I32), scale_rows[0, 4 * q : 4 * q + 4, :].bitcast(I32)
                )

        load_rows(x_rows[0], xt, 0)
        nc.sync.dma_start(offsets[:], offs)
        load_rows(x_rows[1], xt, 1)
        load_scale_rows(cx_plane, cx_scales)
        load_rows(x_rows[2], xt, 2)
        load_rows(x_rows[3], xt, 3)
        load_rows(w_rows[0], wt, 0)
        load_scale_rows(wc_plane, wc_scales)
        load_rows(w_rows[1], wt, 1)
        load_rows(w_rows[2], wt, 2)
        nc.sync.dma_start(cx_codes[:].bitcast(I32), cx_words[0].bitcast(I32))
        wc_flat = wc_words[0].rearrange("p n r -> p (n r)")
        nc.sync.dma_start(wc_codes[0][:].bitcast(I32), wc_flat[:, 0 : 2 * N].bitcast(I32))
        load_rows(w_rows[3], wt, 3)
        nc.sync.dma_start(wc_codes[1][:].bitcast(I32), wc_flat[:, 2 * N :].bitcast(I32))

        def make_operand(row_tiles, codes, plane):
            grouped = ring.tile([P, len(row_tiles) * 4 * P], BF16, name="grouped", align_bytes=64)
            for j, rows in enumerate(row_tiles):
                picked = ring.tile([P, I], BF16, name="picked")
                nc.vector.tensor_copy(picked[:].rearrange("p (u g e) -> p g u e", u=2, e=16), rows[:].indirect(offsets[:]))
                pairs = picked[:].bitcast(F32)
                turned = turn.tile([P, 2, P], F32, name="turned")
                for u in range(2):
                    nc.tensor.transpose(turned[:, u, :], pairs[:, u * P : (u + 1) * P], ident[:])
                nc.scalar.copy(
                    grouped[:, j * 4 * P : (j + 1) * 4 * P].bitcast(F32).rearrange("p (r u) -> p r u", u=2),
                    turned[:].rearrange("p u r -> p r u"),
                )
            nc.vector.quantize_mx(out=codes.bitcast(E4M3), scales=plane, in_=grouped[:])

        codes = keep.tile([P, T + N], U32, name="codes", align_bytes=64)
        plane = keep.tile([P, T + N], U8, name="plane", align_bytes=64)
        row_tiles = x_rows + w_rows

        def quantise(b0, b1):
            make_operand(row_tiles[b0:b1], codes[:, b0 * P : b1 * P], plane[:, b0 * P : b1 * P])

        def context_pass(acc, b, t0, t1, start, stop):
            nc.tensor.matmul_mx(
                out=acc,
                lhsT=wc_codes[b // 2][:, 4 * (b % 2) * P : 4 * (b % 2 + 1) * P].bitcast(E4M3),
                lhsT_scale=wc_plane[:, b * P : (b + 1) * P],
                rhs=cx_codes[:, 2 * t0 : 2 * t1].bitcast(E2M1),
                rhs_scale=cx_plane[:, t0:t1],
                start=start,
                stop=stop,
            )

        def picked_pass(acc, b, t0, t1, start):
            nc.tensor.matmul_mx(
                out=acc,
                lhsT=codes[:, T + b * P : T + (b + 1) * P].bitcast(E4M3),
                lhsT_scale=plane[:, T + b * P : T + (b + 1) * P],
                rhs=codes[:, t0:t1].bitcast(E4M3),
                rhs_scale=plane[:, t0:t1],
                start=start,
                stop=not start,
            )

        def store_block(acc, b):
            result = keep.tile([P, T], F32, name="result%d" % b)
            nc.scalar.copy(result[:], acc[:])
            nc.sync.dma_start(out[b * P : (b + 1) * P, :], result[:])

        accs = [sums.tile([P, T], F32, name="acc%d" % b) for b in range(BLOCKS - 1)]
        half = T // 2
        last = BLOCKS - 1
        halves = [sums.tile([P, half], F32, name="acc_half%d" % h) for h in range(2)]
        quantise(0, 1)
        quantise(1, 3)
        quantise(3, 5)
        picked_pass(accs[0][:], 0, 0, T, True)
        quantise(5, 7)
        context_pass(accs[0][:], 0, 0, T, False, True)
        store_block(accs[0], 0)
        context_pass(accs[1][:], 1, 0, T, True, False)
        picked_pass(accs[1][:], 1, 0, T, False)
        store_block(accs[1], 1)
        picked_pass(accs[2][:], 2, 0, T, True)
        quantise(7, 8)
        context_pass(accs[2][:], 2, 0, T, False, True)
        store_block(accs[2], 2)
        for h in range(2):
            for s in range(2):
                t0 = h * half + s * P
                context_pass(halves[h][:, s * P : (s + 1) * P], last, t0, t0 + P, s == 0, False)
        for h in range(2):
            picked_pass(halves[h][:], last, h * half, (h + 1) * half, False)
            result = keep.tile([P, half], F32, name="result_half%d" % h)
            if h == 0:
                nc.vector.tensor_copy(result[:], halves[h][:])
                nc.sync.dma_start(out[last * P :, 0:half], result[:])
            else:
                nc.scalar.copy(result[:], halves[h][:])
                nc.scalar.dma_start(out[last * P :, half:T], result[:])
